import numpy as np
import ml_dtypes


def mxq(x, axis, fmt="e4m3"):
    dtype, down = {"e4m3": (ml_dtypes.float8_e4m3fn, 7), "e5m2": (ml_dtypes.float8_e5m2, 14)}[fmt]
    v = np.moveaxis(np.asarray(x, np.float32).astype(ml_dtypes.bfloat16).astype(np.float64), axis, -1)
    blocks = v.reshape(v.shape[:-1] + (-1, 32))
    amax = np.abs(blocks).max(-1, keepdims=True)
    byte = np.maximum(np.where(amax > 0, np.frexp(amax)[1] - 1 + 127, 0) - down, 1)
    scale = np.exp2(byte - 127.0)
    codes = (blocks / scale).astype(np.float32).astype(dtype).astype(np.float64)
    return np.moveaxis((codes * scale).reshape(v.shape), -1, axis)


WIDE = False


def mx_kscale(k):
    if not WIDE:
        return np.ones(k)
    levels = np.array([10, -10, 5, -5, 0])
    if k % 512:
        return np.exp2(np.random.permutation(np.resize(levels, k // 32))).repeat(32)
    a = np.empty((k // 512, 16))
    for p in range(k // 512):
        a[p, :8] = np.random.permutation(np.resize(levels, 8))
        for g in range(8):
            far = levels[np.abs(levels - a[p, g]) >= 10]
            a[p, g + 8] = far[np.random.randint(len(far))]
    return np.exp2(a.ravel()).repeat(32)


def f64(x):
    return np.asarray(x).astype(np.float64)


def striped(idx):
    return np.tile(idx.reshape(-1, 16).T, (8, 1)).astype(np.uint16)


def unstriped(offs):
    return offs[:16].T.reshape(-1).astype(np.int64)


E2M1 = np.array([0.0, 0.5, 1.0, 1.5, 2.0, 3.0, 4.0, 6.0, -0.0, -0.5, -1.0, -1.5, -2.0, -3.0, -4.0, -6.0])


def pack_weight(w, fmt):
    k, n = w.shape
    w = f64(np.asarray(w, np.float32).astype(ml_dtypes.bfloat16)).reshape(k // 32, 32, n)
    amax = np.abs(w).max(1)
    if fmt == "e4m3":
        byte = np.frexp(amax)[1] - 1 + 127 - 7
    else:
        mant, ex = np.frexp(amax / 6.0)
        byte = np.where(mant > 0.5, ex, ex - 1) + 127
    byte = np.clip(np.where(amax > 0, byte, 1), 1, 254)
    scaled = (w * np.exp2(127.0 - byte)[:, None, :]).reshape(k, n).astype(np.float32)
    by_word = np.ascontiguousarray(scaled.reshape(k // 512, 128, 4, n).transpose(0, 1, 3, 2))
    if fmt == "e4m3":
        words = by_word.astype(ml_dtypes.float8_e4m3fn).view(np.uint8)
    else:
        c = by_word.astype(ml_dtypes.float4_e2m1fn).view(np.uint8) & 0xF
        words = (c[..., 0::2] | (c[..., 1::2] << 4)).reshape(k // 512, 128, 2 * n)
    return np.ascontiguousarray(words), np.ascontiguousarray(byte.astype(np.uint8).reshape(k // 512, 16, n))


def unpack_weight(words, scales, fmt):
    g, _, n = scales.shape
    words = np.ascontiguousarray(words).reshape(g, 128, n, -1)
    if fmt == "e4m3":
        vals = words.view(ml_dtypes.float8_e4m3fn).astype(np.float64)
    else:
        nib = np.empty((g, 128, n, 4), np.uint8)
        nib[..., 0::2] = words & 0xF
        nib[..., 1::2] = words >> 4
        vals = E2M1[nib]
    vals = vals * np.repeat(np.exp2(scales.astype(np.float64) - 127.0), 8, axis=1)[..., None]
    return vals.transpose(0, 1, 3, 2).reshape(g * 512, n)


def gelu(v):
    return 0.5 * v * (1.0 + np.tanh(np.sqrt(2.0 / np.pi) * (v + 0.044715 * v**3)))


K, T, E, C, H, N = 2048, 512, 2, 256, 512, 256


def by_expert(wq, xq):
    return np.concatenate([wq[e].T @ xq[:, e * C:(e + 1) * C] for e in range(E)], axis=1)


def setup_inputs():
    n = np.random.standard_normal
    s = mx_kscale(K)[:, None]
    u = mx_kscale(H)
    x = pack_weight(n((K, T)) * s, "e4m3")
    return {
        "x_words": x[0],
        "x_scales": x[1],
        "w1": (n((E, K, H)) / np.sqrt(K) / s[None] * u[None, None, :]).astype(np.float32),
        "w2": (n((E, H, N)) / np.sqrt(H) / u[None, :, None]).astype(np.float32),
        "gate": np.tile(np.random.uniform(0.2, 1.0, E * C), (N, 1)).astype(np.float32),
        "offs": striped(np.random.permutation(T)[:E * C]),
        "dst": striped(np.random.permutation(T)[:E * C]),
    }


def reference(x_words, x_scales, w1, w2, gate, offs, dst):
    idx = unstriped(offs)
    xq = unpack_weight(x_words, x_scales, "e4m3")[:, idx]
    h = gelu(by_expert(mxq(f64(w1), 1, "e4m3"), xq))
    y = by_expert(mxq(f64(w2), 1, "e4m3"), mxq(h, 0, "e4m3"))
    out = np.zeros((N, T))
    out[:, unstriped(dst)] = f64(gate) * y
    return out

@@ -1,0 +1,227 @@
+from contextlib import ExitStack
+
+import concourse.mybir as mybir
+
+K, T, E, C, H, N = 2048, 512, 2, 256, 512, 256
+FLOPS = 2 * E * C * (K * H + H * N)
+
+F32 = mybir.dt.float32
+BF16 = mybir.dt.bfloat16
+I32 = mybir.dt.int32
+U32 = mybir.dt.uint32
+U16 = mybir.dt.uint16
+U8 = mybir.dt.uint8
+FP8X4 = mybir.dt.float8_e4m3fn_x4
+GELU = mybir.ActivationFunctionType.Gelu_apprx_tanh
+MULT = mybir.AluOpType.mult
+
+P = 128
+PACK = 4
+K_PASS = P * PACK
+PASSES = K // K_PASS
+HALF = C // 2
+BLOCKS = N // P
+SCALAR_SHARE = [[128, 128, 96, 44], [128, 96, 64, 44]]
+PARTS = [2, 2]
+
+
+def tile_moe_two_mlp_gelu_kernel(
+    tc, x_words, x_scales, w1, w2, gate, offs, dst, out
+):
+    nc = tc.nc
+    with ExitStack() as ctx:
+        sb = ctx.enter_context(tc.tile_pool(name="sb", bufs=1))
+        ps = ctx.enter_context(tc.psum_pool(name="ps", bufs=1))
+
+        def tile(shape, dtype, name):
+            return sb.tile(shape, dtype, name=name, align_bytes=64)
+
+        banks = [[ps.tile([P, 512], F32, name=f"bank{s}_{t}") for t in range(PACK)] for s in range(2)]
+
+        w1_raw = [[tile([P, PACK, H], F32, f"w1_raw{e}_{o}") for o in range(PASSES)] for e in range(E)]
+        w2_raw = [tile([P, PACK, N], F32, f"w2_raw{e}") for e in range(E)]
+        gate_sb = [tile([P, C], F32, f"gate{e}") for e in range(E)]
+        words = [tile([P, 2, T], I32, f"words{u}") for u in range(2)]
+        scales = tile([P, T], U8, "scales")
+        offs_sb = sb.tile([P, E * C // 16], U16, name="offs_sb")
+        dst_sb = sb.tile([P, E * C // 16], U16, name="dst_sb")
+        result = [tile([P, T], F32, f"result{b}") for b in range(BLOCKS)]
+        warm = tile([P, 8], F32, "warm")
+
+        def load_w1(e, o):
+            rows = w1[e, o * K_PASS:(o + 1) * K_PASS, :]
+            nc.sync.dma_start(out=w1_raw[e][o][:], in_=rows.rearrange("(p j) c -> p j c", j=PACK))
+
+        def load_tail(e):
+            nc.sync.dma_start(out=w2_raw[e][:], in_=w2[e].rearrange("(p j) n -> p j n", j=PACK))
+            nc.sync.dma_start(out=gate_sb[e][:], in_=gate[0:P, e * C:(e + 1) * C])
+
+        nc.vector.memset(scales[:].bitcast(I32), 0)
+        nc.vector.memset(warm[:], 0.0)
+        nc.scalar.activation(warm[:, 4:8], warm[:, 0:4], GELU)
+        nc.sync.dma_start(offs_sb[:], offs)
+        for q in range(4):
+            nc.scalar.dma_start(
+                out=scales[32 * q:32 * q + 16, :].bitcast(I32),
+                in_=x_scales[:, 4 * q:4 * q + 4, :].bitcast(I32),
+            )
+        for u in range(2):
+            src = x_words[2 * u:2 * u + 2].rearrange("o p t r -> p o (t r)").bitcast(I32)
+            nc.sync.dma_start(out=words[u][:], in_=src)
+            load_w1(0, u)
+        for o in range(2, PASSES):
+            load_w1(0, o)
+        nc.sync.dma_start(dst_sb[:], dst)
+        load_tail(0)
+        for o in range(PASSES):
+            load_w1(1, o)
+        load_tail(1)
+
+        def slots(listed, first, count):
+            return listed[:, first // 16:(first + count) // 16]
+
+        x_codes = [[tile([P, C], U32, f"x_codes{e}_{o}") for o in range(PASSES)] for e in range(E)]
+        x_bytes = [tile([P, C], U8, f"x_bytes{e}") for e in range(E)]
+
+        def gather_bytes(e):
+            nc.vector.tensor_copy(x_bytes[e][:], scales[:].indirect(slots(offs_sb, e * C, C)))
+
+        def gather_words(e, o):
+            window = words[o // 2][:, o % 2, :].bitcast(U32)
+            nc.vector.tensor_copy(x_codes[e][o][:], window.indirect(slots(offs_sb, e * C, C)))
+
+        w1_bf = [[tile([P, PACK, P, PACK], BF16, f"w1_bf{e}_{o}") for o in range(PASSES)] for e in range(E)]
+        w1_codes = [[tile([P, H], U32, f"w1_codes{e}_{o}") for o in range(PASSES)] for e in range(E)]
+        w1_bytes = [[tile([P, H], U8, f"w1_bytes{e}_{o}") for o in range(PASSES)] for e in range(E)]
+
+        def round_w1(e, o):
+            src = w1_raw[e][o][:].rearrange("p j (m t) -> p m j t", t=PACK)
+            to = w1_bf[e][o][:].rearrange("p t m j -> p m j t")
+            share = SCALAR_SHARE[e][o]
+            nc.scalar.copy(to[:, :share], src[:, :share])
+            if share < P:
+                nc.vector.tensor_copy(to[:, share:], src[:, share:])
+
+        def quantize_w1(e, o, parts=1):
+            flat = w1_bf[e][o][:].rearrange("p t m j -> p (t m j)")
+            w = H // parts
+            for i in range(parts):
+                nc.vector.quantize_mx(
+                    out=w1_codes[e][o][:, i * w:(i + 1) * w].bitcast(FP8X4),
+                    scales=w1_bytes[e][o][:, i * w:(i + 1) * w],
+                    in_=flat[:, PACK * i * w:PACK * (i + 1) * w],
+                )
+
+        def first_pass(e, o):
+            width = C // PARTS[e]
+            for s in range(PARTS[e]):
+                cols = slice(s * width, (s + 1) * width)
+                for t in range(PACK):
+                    chans = slice(t * P, (t + 1) * P)
+                    nc.tensor.matmul_mx(
+                        out=banks[s][t][:, :width],
+                        lhsT=w1_codes[e][o][:, chans].bitcast(FP8X4),
+                        lhsT_scale=w1_bytes[e][o][:, chans],
+                        rhs=x_codes[e][o][:, cols].bitcast(FP8X4),
+                        rhs_scale=x_bytes[e][PACK * o:, cols],
+                        start=(o == 0),
+                        stop=(o == PASSES - 1),
+                    )
+
+        w2_bf = [[tile([P, P, PACK], BF16, f"w2_bf{e}_{b}") for b in range(BLOCKS)] for e in range(E)]
+        w2_codes = [[tile([P, P], U32, f"w2_codes{e}_{b}") for b in range(BLOCKS)] for e in range(E)]
+        w2_bytes = [[tile([P, P], U8, f"w2_bytes{e}_{b}") for b in range(BLOCKS)] for e in range(E)]
+
+        def interleave(copy, to, src):
+            copy(to.rearrange("p (c i) j -> p c j i", i=4), src.rearrange("p j (c i) -> p c j i", i=4))
+
+        def quantize(codes, scale_bytes, values):
+            nc.vector.quantize_mx(
+                out=codes[:].bitcast(FP8X4), scales=scale_bytes[:], in_=values[:].rearrange("p c j -> p (c j)")
+            )
+
+        def round_w2(e, b, copy):
+            interleave(copy, w2_bf[e][b][:], w2_raw[e][:, :, b * P:(b + 1) * P])
+
+        def quantize_w2(e, b):
+            quantize(w2_codes[e][b], w2_bytes[e][b], w2_bf[e][b])
+
+        def per_part(dims, dtype, name):
+            return [[tile(dims(C // PARTS[e]), dtype, f"{name}{e}_{s}") for s in range(PARTS[e])] for e in range(E)]
+
+        h_planes = per_part(lambda w: [P, PACK, w], BF16, "h_planes")
+        h_bf = per_part(lambda w: [P, w, PACK], BF16, "h_bf")
+        h_codes = per_part(lambda w: [P, w], U32, "h_codes")
+        h_bytes = per_part(lambda w: [P, w], U8, "h_bytes")
+        y_sb = [[tile([P, C], F32, f"y{e}_{b}") for b in range(BLOCKS)] for e in range(E)]
+
+        def gelu(e, s):
+            for t in range(PACK):
+                nc.scalar.activation(h_planes[e][s][:, t, :], banks[s][t][:, :C // PARTS[e]], GELU)
+
+        def weave_h(e, s):
+            interleave(nc.vector.tensor_copy, h_bf[e][s][:], h_planes[e][s][:])
+
+        def quantize_h(e, s):
+            quantize(h_codes[e][s], h_bytes[e][s], h_bf[e][s])
+
+        def second(e, s, b):
+            width = C // PARTS[e]
+            acc = banks[s][b][:, :width]
+            nc.tensor.matmul_mx(
+                out=acc,
+                lhsT=w2_codes[e][b][:].bitcast(FP8X4),
+                lhsT_scale=w2_bytes[e][b][:],
+                rhs=h_codes[e][s][:].bitcast(FP8X4),
+                rhs_scale=h_bytes[e][s][:],
+                start=True,
+                stop=True,
+            )
+            nc.scalar.copy(y_sb[e][b][:, s * width:(s + 1) * width], acc)
+
+        def scatter(e, b, first, count):
+            nc.vector.tensor_tensor(
+                result[b][:].indirect(slots(dst_sb, e * C + first, count)),
+                y_sb[e][b][:, first:first + count],
+                gate_sb[e][:, first:first + count],
+                MULT,
+            )
+
+        def finish(e, first_copy, second_copy):
+            gelu(e, 0)
+            round_w2(e, 0, first_copy)
+            gelu(e, 1)
+            quantize_w2(e, 0)
+            weave_h(e, 0)
+            round_w2(e, 1, second_copy)
+            quantize_h(e, 0)
+            weave_h(e, 1)
+            second(e, 0, 0)
+            quantize_w2(e, 1)
+            quantize_h(e, 1)
+            second(e, 1, 0)
+            second(e, 0, 1)
+            second(e, 1, 1)
+            scatter(e, 0, 0, HALF)
+            scatter(e, 0, HALF, HALF)
+            scatter(e, 1, 0, C)
+
+        for e in range(E):
+            gather_bytes(e)
+            gather_words(e, 0)
+            gather_words(e, 1)
+        for e in range(E):
+            for o in range(PASSES):
+                round_w1(e, o)
+                if e == 0 and o == 0:
+                    for later in range(2, PASSES):
+                        for expert in range(E):
+                            gather_words(expert, later)
+                quantize_w1(e, o, parts=4 if o == PASSES - 1 else 1)
+                first_pass(e, o)
+            if e == 0:
+                finish(e, nc.scalar.copy, nc.vector.tensor_copy)
+            else:
+                finish(e, nc.vector.tensor_copy, nc.scalar.copy)
+        for b in range(BLOCKS):
+            nc.sync.dma_start(out=out[b * P:(b + 1) * P, :], in_=result[b][:])

@@ -19,10 +19,9 @@ P = 128
 PACK = 4
 K_PASS = P * PACK
 PASSES = K // K_PASS
-HALF = C // 2
+GROUPS = C // P
 BLOCKS = N // P
-SCALAR_SHARE = [[128, 128, 96, 44], [128, 96, 64, 44]]
-PARTS = [2, 2]
+VECTOR_SHARE = [[0, 0, 0, 84], [0, 0, 24, 84]]
 
 
 def tile_moe_two_mlp_gelu_kernel(
@@ -33,15 +32,18 @@ def tile_moe_two_mlp_gelu_kernel(
         sb = ctx.enter_context(tc.tile_pool(name="sb", bufs=1))
         ps = ctx.enter_context(tc.psum_pool(name="ps", bufs=1))
 
-        def tile(shape, dtype, name):
-            return sb.tile(shape, dtype, name=name, align_bytes=64)
+        def tile(shape, dtype, name, after=None):
+            return sb.tile(shape, dtype, name=name, tag=after or name, align_bytes=64)
 
-        banks = [[ps.tile([P, 512], F32, name=f"bank{s}_{t}") for t in range(PACK)] for s in range(2)]
+        def tiles(shape, dtype, name, count):
+            return [[tile(shape, dtype, f"{name}{e}_{i}") for i in range(count)] for e in range(E)]
 
-        w1_raw = [[tile([P, PACK, H], F32, f"w1_raw{e}_{o}") for o in range(PASSES)] for e in range(E)]
+        banks = [[ps.tile([P, 512], F32, name=f"bank{s}_{i}") for i in range(PACK)] for s in range(GROUPS)]
+
+        w1_raw = tiles([P, PACK, H], F32, "w1_raw", PASSES)
         w2_raw = [tile([P, PACK, N], F32, f"w2_raw{e}") for e in range(E)]
         gate_sb = [tile([P, C], F32, f"gate{e}") for e in range(E)]
-        words = [tile([P, 2, T], I32, f"words{u}") for u in range(2)]
+        words = [tile([P, T], I32, f"words{o}") for o in range(PASSES)]
         scales = tile([P, T], U8, "scales")
         offs_sb = sb.tile([P, E * C // 16], U16, name="offs_sb")
         dst_sb = sb.tile([P, E * C // 16], U16, name="dst_sb")
@@ -52,8 +54,10 @@ def tile_moe_two_mlp_gelu_kernel(
             rows = w1[e, o * K_PASS:(o + 1) * K_PASS, :]
             nc.sync.dma_start(out=w1_raw[e][o][:], in_=rows.rearrange("(p j) c -> p j c", j=PACK))
 
-        def load_tail(e):
+        def load_w2(e):
             nc.sync.dma_start(out=w2_raw[e][:], in_=w2[e].rearrange("(p j) n -> p j n", j=PACK))
+
+        def load_gate(e):
             nc.sync.dma_start(out=gate_sb[e][:], in_=gate[0:P, e * C:(e + 1) * C])
 
         nc.vector.memset(scales[:].bitcast(I32), 0)
@@ -65,109 +69,112 @@ def tile_moe_two_mlp_gelu_kernel(
                 out=scales[32 * q:32 * q + 16, :].bitcast(I32),
                 in_=x_scales[:, 4 * q:4 * q + 4, :].bitcast(I32),
             )
-        for u in range(2):
-            src = x_words[2 * u:2 * u + 2].rearrange("o p t r -> p o (t r)").bitcast(I32)
-            nc.sync.dma_start(out=words[u][:], in_=src)
-            load_w1(0, u)
-        for o in range(2, PASSES):
-            load_w1(0, o)
-        nc.sync.dma_start(dst_sb[:], dst)
-        load_tail(0)
         for o in range(PASSES):
+            nc.sync.dma_start(out=words[o][:], in_=x_words[o].rearrange("p t r -> p (t r)").bitcast(I32))
+            load_w1(0, o)
+        load_w2(0)
+        load_w1(1, 0)
+        load_gate(0)
+        nc.sync.dma_start(dst_sb[:], dst)
+        for o in range(1, PASSES):
             load_w1(1, o)
-        load_tail(1)
+        load_w2(1)
+        load_gate(1)
 
         def slots(listed, first, count):
             return listed[:, first // 16:(first + count) // 16]
 
-        x_codes = [[tile([P, C], U32, f"x_codes{e}_{o}") for o in range(PASSES)] for e in range(E)]
+        x_codes = tiles([P, C], U32, "x_codes", PASSES)
         x_bytes = [tile([P, C], U8, f"x_bytes{e}") for e in range(E)]
 
         def gather_bytes(e):
             nc.vector.tensor_copy(x_bytes[e][:], scales[:].indirect(slots(offs_sb, e * C, C)))
 
         def gather_words(e, o):
-            window = words[o // 2][:, o % 2, :].bitcast(U32)
+            window = words[o][:].bitcast(U32)
             nc.vector.tensor_copy(x_codes[e][o][:], window.indirect(slots(offs_sb, e * C, C)))
 
-        w1_bf = [[tile([P, PACK, P, PACK], BF16, f"w1_bf{e}_{o}") for o in range(PASSES)] for e in range(E)]
-        w1_codes = [[tile([P, H], U32, f"w1_codes{e}_{o}") for o in range(PASSES)] for e in range(E)]
-        w1_bytes = [[tile([P, H], U8, f"w1_bytes{e}_{o}") for o in range(PASSES)] for e in range(E)]
+        def round_rows(copy, to, src):
+            copy(to.rearrange("p (c i) j -> p c j i", i=4), src.rearrange("p j (c i) -> p c j i", i=4))
+
+        def quantize(codes, scale_bytes, values):
+            nc.vector.quantize_mx(out=codes.bitcast(FP8X4), scales=scale_bytes, in_=values.rearrange("p c j -> p (c j)"))
+
+        w1_bf = [[None] * PASSES for e in range(E)]
+        w1_codes = tiles([P, H], U32, "w1_codes", PASSES)
+        w1_bytes = tiles([P, H], U8, "w1_bytes", PASSES)
 
         def round_w1(e, o):
-            src = w1_raw[e][o][:].rearrange("p j (m t) -> p m j t", t=PACK)
-            to = w1_bf[e][o][:].rearrange("p t m j -> p m j t")
-            share = SCALAR_SHARE[e][o]
-            nc.scalar.copy(to[:, :share], src[:, :share])
-            if share < P:
-                nc.vector.tensor_copy(to[:, share:], src[:, share:])
+            share = VECTOR_SHARE[e][o]
+            src = w1_raw[e][o][:].rearrange("p j (m u v) -> p u m j v", u=2, v=2)
+            if o == 0 and e > 0:
+                low = tile([P, 2, P, PACK], BF16, f"w1_bf{e}_low", f"h_bf{e - 1}_0")
+                high = tile([P, 2, P, PACK], BF16, f"w1_bf{e}_high", f"h_planes{e - 1}_1")
+                w1_bf[e][o] = [t[:].rearrange("p v m j -> p (v m) j") for t in (low, high)]
+                for m in range(0, P, P // 2):
+                    ms = slice(m, m + P // 2)
+                    nc.scalar.copy(high[:].rearrange("p v m j -> p m j v")[:, ms], src[:, 1, ms])
+                nc.vector.tensor_copy(low[:].rearrange("p v m j -> p m j v"), src[:, 0])
+                return
+            whole = tile([P, H, PACK], BF16, f"w1_bf{e}_{o}", f"w1_raw{e}_{o - 1}" if o > 0 else None)
+            parts = PACK if o == PASSES - 1 else 1
+            w1_bf[e][o] = [whole[:, i * H // parts:(i + 1) * H // parts, :] for i in range(parts)]
+            to = whole[:].rearrange("p (u v m) j -> p u m j v", u=2, v=2)
+            nc.scalar.copy(to[:, :, share:], src[:, :, share:])
+            if share:
+                nc.vector.tensor_copy(to[:, :, :share], src[:, :, :share])
 
-        def quantize_w1(e, o, parts=1):
-            flat = w1_bf[e][o][:].rearrange("p t m j -> p (t m j)")
-            w = H // parts
-            for i in range(parts):
-                nc.vector.quantize_mx(
-                    out=w1_codes[e][o][:, i * w:(i + 1) * w].bitcast(FP8X4),
-                    scales=w1_bytes[e][o][:, i * w:(i + 1) * w],
-                    in_=flat[:, PACK * i * w:PACK * (i + 1) * w],
-                )
+        def quantize_w1(e, o):
+            width = H // len(w1_bf[e][o])
+            for i, values in enumerate(w1_bf[e][o]):
+                cols = slice(i * width, (i + 1) * width)
+                quantize(w1_codes[e][o][:, cols], w1_bytes[e][o][:, cols], values)
 
         def first_pass(e, o):
-            width = C // PARTS[e]
-            for s in range(PARTS[e]):
-                cols = slice(s * width, (s + 1) * width)
+            for s in range(GROUPS):
+                group = slice(s * P, (s + 1) * P)
                 for t in range(PACK):
-                    chans = slice(t * P, (t + 1) * P)
+                    cols = slice(t * P, (t + 1) * P)
                     nc.tensor.matmul_mx(
-                        out=banks[s][t][:, :width],
-                        lhsT=w1_codes[e][o][:, chans].bitcast(FP8X4),
-                        lhsT_scale=w1_bytes[e][o][:, chans],
-                        rhs=x_codes[e][o][:, cols].bitcast(FP8X4),
-                        rhs_scale=x_bytes[e][PACK * o:, cols],
+                        out=banks[s][t][:, :P],
+                        lhsT=w1_codes[e][o][:, cols].bitcast(FP8X4),
+                        lhsT_scale=w1_bytes[e][o][:, cols],
+                        rhs=x_codes[e][o][:, group].bitcast(FP8X4),
+                        rhs_scale=x_bytes[e][PACK * o:, group],
                         start=(o == 0),
                         stop=(o == PASSES - 1),
                     )
 
-        w2_bf = [[tile([P, P, PACK], BF16, f"w2_bf{e}_{b}") for b in range(BLOCKS)] for e in range(E)]
-        w2_codes = [[tile([P, P], U32, f"w2_codes{e}_{b}") for b in range(BLOCKS)] for e in range(E)]
-        w2_bytes = [[tile([P, P], U8, f"w2_bytes{e}_{b}") for b in range(BLOCKS)] for e in range(E)]
+        w2_bf = [[None] * BLOCKS for e in range(E)]
+        w2_codes = tiles([P, P], U32, "w2_codes", BLOCKS)
+        w2_bytes = tiles([P, P], U8, "w2_bytes", BLOCKS)
 
-        def interleave(copy, to, src):
-            copy(to.rearrange("p (c i) j -> p c j i", i=4), src.rearrange("p j (c i) -> p c j i", i=4))
-
-        def quantize(codes, scale_bytes, values):
-            nc.vector.quantize_mx(
-                out=codes[:].bitcast(FP8X4), scales=scale_bytes[:], in_=values[:].rearrange("p c j -> p (c j)")
-            )
-
-        def round_w2(e, b, copy):
-            interleave(copy, w2_bf[e][b][:], w2_raw[e][:, :, b * P:(b + 1) * P])
+        def round_w2(e, b):
+            after = f"w1_raw{e}_{PASSES - 2}" if b == 0 else (f"h_bf{e}_0" if e == E - 1 else f"w1_raw{e}_{PASSES - 1}")
+            w2_bf[e][b] = tile([P, P, PACK], BF16, f"w2_bf{e}_{b}", after)
+            round_rows(nc.vector.tensor_copy, w2_bf[e][b][:], w2_raw[e][:, :, b * P:(b + 1) * P])
 
         def quantize_w2(e, b):
-            quantize(w2_codes[e][b], w2_bytes[e][b], w2_bf[e][b])
+            quantize(w2_codes[e][b][:], w2_bytes[e][b][:], w2_bf[e][b][:])
 
-        def per_part(dims, dtype, name):
-            return [[tile(dims(C // PARTS[e]), dtype, f"{name}{e}_{s}") for s in range(PARTS[e])] for e in range(E)]
-
-        h_planes = per_part(lambda w: [P, PACK, w], BF16, "h_planes")
-        h_bf = per_part(lambda w: [P, w, PACK], BF16, "h_bf")
-        h_codes = per_part(lambda w: [P, w], U32, "h_codes")
-        h_bytes = per_part(lambda w: [P, w], U8, "h_bytes")
-        y_sb = [[tile([P, C], F32, f"y{e}_{b}") for b in range(BLOCKS)] for e in range(E)]
+        h_planes = tiles([P, PACK, P], BF16, "h_planes", GROUPS)
+        h_bf = tiles([P, P, PACK], BF16, "h_bf", GROUPS)
+        h_codes = tiles([P, P], U32, "h_codes", GROUPS)
+        h_bytes = tiles([P, P], U8, "h_bytes", GROUPS)
+        y_sb = tiles([P, C], F32, "y", BLOCKS)
 
         def gelu(e, s):
             for t in range(PACK):
-                nc.scalar.activation(h_planes[e][s][:, t, :], banks[s][t][:, :C // PARTS[e]], GELU)
+                nc.scalar.activation(h_planes[e][s][:, t, :], banks[s][t][:, :P], GELU)
 
-        def weave_h(e, s):
-            interleave(nc.vector.tensor_copy, h_bf[e][s][:], h_planes[e][s][:])
+        def weave_h(e, s, copy):
+            round_rows(copy, h_bf[e][s][:], h_planes[e][s][:])
 
         def quantize_h(e, s):
-            quantize(h_codes[e][s], h_bytes[e][s], h_bf[e][s])
+            quantize(h_codes[e][s][:], h_bytes[e][s][:], h_bf[e][s][:])
 
         def second(e, s, b):
-            width = C // PARTS[e]
-            acc = banks[s][b][:, :width]
+            acc = banks[s][b][:, :P]
             nc.tensor.matmul_mx(
                 out=acc,
                 lhsT=w2_codes[e][b][:].bitcast(FP8X4),
@@ -177,7 +184,7 @@ def tile_moe_two_mlp_gelu_kernel(
                 start=True,
                 stop=True,
             )
-            nc.scalar.copy(y_sb[e][b][:, s * width:(s + 1) * width], acc)
+            nc.scalar.copy(y_sb[e][b][:, s * P:(s + 1) * P], acc)
 
         def scatter(e, b, first, count):
             nc.vector.tensor_tensor(
@@ -187,41 +194,40 @@ def tile_moe_two_mlp_gelu_kernel(
                 MULT,
             )
 
-        def finish(e, first_copy, second_copy):
+        def finish(e):
             gelu(e, 0)
-            round_w2(e, 0, first_copy)
+            round_w2(e, 0)
+            if e < E - 1:
+                round_w2(e, 1)
             gelu(e, 1)
             quantize_w2(e, 0)
-            weave_h(e, 0)
-            round_w2(e, 1, second_copy)
+            if e < E - 1:
+                quantize_w2(e, 1)
+            weave_h(e, 0, nc.vector.tensor_copy)
+            weave_h(e, 1, nc.scalar.copy)
             quantize_h(e, 0)
-            weave_h(e, 1)
             second(e, 0, 0)
-            quantize_w2(e, 1)
+            if e == E - 1:
+                round_w2(e, 1)
+                quantize_w2(e, 1)
             quantize_h(e, 1)
-            second(e, 1, 0)
             second(e, 0, 1)
+            second(e, 1, 0)
             second(e, 1, 1)
-            scatter(e, 0, 0, HALF)
-            scatter(e, 0, HALF, HALF)
-            scatter(e, 1, 0, C)
+            for s in range(GROUPS):
+                for b in range(BLOCKS):
+                    scatter(e, b, s * P, P)
 
         for e in range(E):
             gather_bytes(e)
-            gather_words(e, 0)
-            gather_words(e, 1)
         for e in range(E):
             for o in range(PASSES):
+                if e == 0:
+                    for expert in range(E):
+                        gather_words(expert, o)
                 round_w1(e, o)
-                if e == 0 and o == 0:
-                    for later in range(2, PASSES):
-                        for expert in range(E):
-                            gather_words(expert, later)
-                quantize_w1(e, o, parts=4 if o == PASSES - 1 else 1)
+                quantize_w1(e, o)
                 first_pass(e, o)
-            if e == 0:
-                finish(e, nc.scalar.copy, nc.vector.tensor_copy)
-            else:
-                finish(e, nc.vector.tensor_copy, nc.scalar.copy)
+            finish(e)
         for b in range(BLOCKS):
             nc.sync.dma_start(out=out[b * P:(b + 1) * P, :], in_=result[b][:])

@@ -95,7 +95,7 @@ def tile_moe_two_mlp_gelu_kernel(
             nc.vector.tensor_copy(x_codes[e][o][:], window.indirect(slots(offs_sb, e * C, C)))
 
         def round_rows(copy, to, src):
-            copy(to.rearrange("p (c i) j -> p c j i", i=4), src.rearrange("p j (c i) -> p c j i", i=4))
+            copy(to, src.rearrange("p j c -> p c j"))
 
         def quantize(codes, scale_bytes, values):
             nc.vector.quantize_mx(out=codes.bitcast(FP8X4), scales=scale_bytes, in_=values.rearrange("p c j -> p (c j)"))
@@ -106,23 +106,23 @@ def tile_moe_two_mlp_gelu_kernel(
 
         def round_w1(e, o):
             share = VECTOR_SHARE[e][o]
-            src = w1_raw[e][o][:].rearrange("p j (m u v) -> p u m j v", u=2, v=2)
+            src = w1_raw[e][o][:].rearrange("p (a b) (m t) -> p m a t b", b=2, t=PACK)
             if o == 0 and e > 0:
                 low = tile([P, 2, P, PACK], BF16, f"w1_bf{e}_low", f"h_bf{e - 1}_0")
                 high = tile([P, 2, P, PACK], BF16, f"w1_bf{e}_high", f"h_planes{e - 1}_1")
                 w1_bf[e][o] = [t[:].rearrange("p v m j -> p (v m) j") for t in (low, high)]
                 for m in range(0, P, P // 2):
                     ms = slice(m, m + P // 2)
-                    nc.scalar.copy(high[:].rearrange("p v m j -> p m j v")[:, ms], src[:, 1, ms])
-                nc.vector.tensor_copy(low[:].rearrange("p v m j -> p m j v"), src[:, 0])
+                    nc.scalar.copy(high[:].rearrange("p t m (a b) -> p m a t b", b=2)[:, ms], src[:, ms, :, 2:])
+                nc.vector.tensor_copy(low[:].rearrange("p t m (a b) -> p m a t b", b=2), src[:, :, :, :2])
                 return
             whole = tile([P, H, PACK], BF16, f"w1_bf{e}_{o}", f"w1_raw{e}_{o - 1}" if o > 0 else None)
             parts = PACK if o == PASSES - 1 else 1
             w1_bf[e][o] = [whole[:, i * H // parts:(i + 1) * H // parts, :] for i in range(parts)]
-            to = whole[:].rearrange("p (u v m) j -> p u m j v", u=2, v=2)
-            nc.scalar.copy(to[:, :, share:], src[:, :, share:])
+            to = whole[:].rearrange("p (t m) (a b) -> p m a t b", b=2, t=PACK)
+            nc.scalar.copy(to[:, share:], src[:, share:])
             if share:
-                nc.vector.tensor_copy(to[:, :, :share], src[:, :, :share])
+                nc.vector.tensor_copy(to[:, :share], src[:, :share])
 
         def quantize_w1(e, o):
             width = H // len(w1_bf[e][o])
@@ -149,10 +149,9 @@ def tile_moe_two_mlp_gelu_kernel(
         w2_codes = tiles([P, P], U32, "w2_codes", BLOCKS)
         w2_bytes = tiles([P, P], U8, "w2_bytes", BLOCKS)
 
-        def round_w2(e, b):
-            after = f"w1_raw{e}_{PASSES - 2}" if b == 0 else (f"h_bf{e}_0" if e == E - 1 else f"w1_raw{e}_{PASSES - 1}")
-            w2_bf[e][b] = tile([P, P, PACK], BF16, f"w2_bf{e}_{b}", after)
-            round_rows(nc.vector.tensor_copy, w2_bf[e][b][:], w2_raw[e][:, :, b * P:(b + 1) * P])
+        def round_w2(e, b, copy):
+            w2_bf[e][b] = tile([P, P, PACK], BF16, f"w2_bf{e}_{b}", f"w1_raw{e}_{PASSES - 1 - b}")
+            round_rows(copy, w2_bf[e][b][:], w2_raw[e][:, :, b * P:(b + 1) * P])
 
         def quantize_w2(e, b):
             quantize(w2_codes[e][b][:], w2_bytes[e][b][:], w2_bf[e][b][:])
@@ -195,28 +194,23 @@ def tile_moe_two_mlp_gelu_kernel(
             )
 
         def finish(e):
+            round_w2(e, 0, nc.scalar.copy)
+            round_w2(e, 1, nc.vector.tensor_copy)
             gelu(e, 0)
-            round_w2(e, 0)
-            if e < E - 1:
-                round_w2(e, 1)
             gelu(e, 1)
             quantize_w2(e, 0)
-            if e < E - 1:
-                quantize_w2(e, 1)
             weave_h(e, 0, nc.vector.tensor_copy)
-            weave_h(e, 1, nc.scalar.copy)
+            quantize_w2(e, 1)
             quantize_h(e, 0)
             second(e, 0, 0)
-            if e == E - 1:
-                round_w2(e, 1)
-                quantize_w2(e, 1)
+            weave_h(e, 1, nc.scalar.copy)
             quantize_h(e, 1)
-            second(e, 0, 1)
             second(e, 1, 0)
+            second(e, 0, 1)
             second(e, 1, 1)
-            for s in range(GROUPS):
-                for b in range(BLOCKS):
-                    scatter(e, b, s * P, P)
+            scatter(e, 0, 0, P)
+            scatter(e, 0, P, P)
+            scatter(e, 1, 0, C)
 
         for e in range(E):
             gather_bytes(e)

from contextlib import ExitStack

import concourse.mybir as mybir

K, T, E, C, H, N = 2048, 512, 2, 256, 512, 256
FLOPS = 2 * E * C * (K * H + H * N)

F32 = mybir.dt.float32
BF16 = mybir.dt.bfloat16
I32 = mybir.dt.int32
U32 = mybir.dt.uint32
U16 = mybir.dt.uint16
U8 = mybir.dt.uint8
FP8X4 = mybir.dt.float8_e4m3fn_x4
GELU = mybir.ActivationFunctionType.Gelu_apprx_tanh
MULT = mybir.AluOpType.mult

P = 128
PACK = 4
K_PASS = P * PACK
PASSES = K // K_PASS
GROUPS = C // P
BLOCKS = N // P
VECTOR_SHARE = [[0, 0, 0, 84], [0, 0, 24, 84]]


def tile_moe_two_mlp_gelu_kernel(
    tc, x_words, x_scales, w1, w2, gate, offs, dst, out
):
    nc = tc.nc
    with ExitStack() as ctx:
        sb = ctx.enter_context(tc.tile_pool(name="sb", bufs=1))
        ps = ctx.enter_context(tc.psum_pool(name="ps", bufs=1))

        def tile(shape, dtype, name, after=None):
            return sb.tile(shape, dtype, name=name, tag=after or name, align_bytes=64)

        def tiles(shape, dtype, name, count):
            return [[tile(shape, dtype, f"{name}{e}_{i}") for i in range(count)] for e in range(E)]

        banks = [[ps.tile([P, 512], F32, name=f"bank{s}_{i}") for i in range(PACK)] for s in range(GROUPS)]

        w1_raw = tiles([P, PACK, H], F32, "w1_raw", PASSES)
        w2_raw = [tile([P, PACK, N], F32, f"w2_raw{e}") for e in range(E)]
        gate_sb = [tile([P, C], F32, f"gate{e}") for e in range(E)]
        words = [tile([P, T], I32, f"words{o}") for o in range(PASSES)]
        scales = tile([P, T], U8, "scales")
        offs_sb = sb.tile([P, E * C // 16], U16, name="offs_sb")
        dst_sb = sb.tile([P, E * C // 16], U16, name="dst_sb")
        result = [tile([P, T], F32, f"result{b}") for b in range(BLOCKS)]
        warm = tile([P, 8], F32, "warm")

        def load_w1(e, o):
            rows = w1[e, o * K_PASS:(o + 1) * K_PASS, :]
            nc.sync.dma_start(out=w1_raw[e][o][:], in_=rows.rearrange("(p j) c -> p j c", j=PACK))

        def load_w2(e):
            nc.sync.dma_start(out=w2_raw[e][:], in_=w2[e].rearrange("(p j) n -> p j n", j=PACK))

        def load_gate(e):
            nc.sync.dma_start(out=gate_sb[e][:], in_=gate[0:P, e * C:(e + 1) * C])

        nc.vector.memset(scales[:].bitcast(I32), 0)
        nc.vector.memset(warm[:], 0.0)
        nc.scalar.activation(warm[:, 4:8], warm[:, 0:4], GELU)
        nc.sync.dma_start(offs_sb[:], offs)
        for q in range(4):
            nc.scalar.dma_start(
                out=scales[32 * q:32 * q + 16, :].bitcast(I32),
                in_=x_scales[:, 4 * q:4 * q + 4, :].bitcast(I32),
            )
        for o in range(PASSES):
            nc.sync.dma_start(out=words[o][:], in_=x_words[o].rearrange("p t r -> p (t r)").bitcast(I32))
            load_w1(0, o)
        load_w2(0)
        load_w1(1, 0)
        load_gate(0)
        nc.sync.dma_start(dst_sb[:], dst)
        for o in range(1, PASSES):
            load_w1(1, o)
        load_w2(1)
        load_gate(1)

        def slots(listed, first, count):
            return listed[:, first // 16:(first + count) // 16]

        x_codes = tiles([P, C], U32, "x_codes", PASSES)
        x_bytes = [tile([P, C], U8, f"x_bytes{e}") for e in range(E)]

        def gather_bytes(e):
            nc.vector.tensor_copy(x_bytes[e][:], scales[:].indirect(slots(offs_sb, e * C, C)))

        def gather_words(e, o):
            window = words[o][:].bitcast(U32)
            nc.vector.tensor_copy(x_codes[e][o][:], window.indirect(slots(offs_sb, e * C, C)))

        def round_rows(copy, to, src):
            copy(to, src.rearrange("p j c -> p c j"))

        def quantize(codes, scale_bytes, values):
            nc.vector.quantize_mx(out=codes.bitcast(FP8X4), scales=scale_bytes, in_=values.rearrange("p c j -> p (c j)"))

        w1_bf = [[None] * PASSES for e in range(E)]
        w1_codes = tiles([P, H], U32, "w1_codes", PASSES)
        w1_bytes = tiles([P, H], U8, "w1_bytes", PASSES)

        def round_w1(e, o):
            share = VECTOR_SHARE[e][o]
            src = w1_raw[e][o][:].rearrange("p (a b) (m t) -> p m a t b", b=2, t=PACK)
            if o == 0 and e > 0:
                low = tile([P, 2, P, PACK], BF16, f"w1_bf{e}_low", f"h_bf{e - 1}_0")
                high = tile([P, 2, P, PACK], BF16, f"w1_bf{e}_high", f"h_planes{e - 1}_1")
                w1_bf[e][o] = [t[:].rearrange("p v m j -> p (v m) j") for t in (low, high)]
                for m in range(0, P, P // 2):
                    ms = slice(m, m + P // 2)
                    nc.scalar.copy(high[:].rearrange("p t m (a b) -> p m a t b", b=2)[:, ms], src[:, ms, :, 2:])
                nc.vector.tensor_copy(low[:].rearrange("p t m (a b) -> p m a t b", b=2), src[:, :, :, :2])
                return
            whole = tile([P, H, PACK], BF16, f"w1_bf{e}_{o}", f"w1_raw{e}_{o - 1}" if o > 0 else None)
            parts = PACK if o == PASSES - 1 else 1
            w1_bf[e][o] = [whole[:, i * H // parts:(i + 1) * H // parts, :] for i in range(parts)]
            to = whole[:].rearrange("p (t m) (a b) -> p m a t b", b=2, t=PACK)
            nc.scalar.copy(to[:, share:], src[:, share:])
            if share:
                nc.vector.tensor_copy(to[:, :share], src[:, :share])

        def quantize_w1(e, o):
            width = H // len(w1_bf[e][o])
            for i, values in enumerate(w1_bf[e][o]):
                cols = slice(i * width, (i + 1) * width)
                quantize(w1_codes[e][o][:, cols], w1_bytes[e][o][:, cols], values)

        def first_pass(e, o):
            for s in range(GROUPS):
                group = slice(s * P, (s + 1) * P)
                for t in range(PACK):
                    cols = slice(t * P, (t + 1) * P)
                    nc.tensor.matmul_mx(
                        out=banks[s][t][:, :P],
                        lhsT=w1_codes[e][o][:, cols].bitcast(FP8X4),
                        lhsT_scale=w1_bytes[e][o][:, cols],
                        rhs=x_codes[e][o][:, group].bitcast(FP8X4),
                        rhs_scale=x_bytes[e][PACK * o:, group],
                        start=(o == 0),
                        stop=(o == PASSES - 1),
                    )

        w2_bf = [[None] * BLOCKS for e in range(E)]
        w2_codes = tiles([P, P], U32, "w2_codes", BLOCKS)
        w2_bytes = tiles([P, P], U8, "w2_bytes", BLOCKS)

        def round_w2(e, b, copy):
            w2_bf[e][b] = tile([P, P, PACK], BF16, f"w2_bf{e}_{b}", f"w1_raw{e}_{PASSES - 1 - b}")
            round_rows(copy, w2_bf[e][b][:], w2_raw[e][:, :, b * P:(b + 1) * P])

        def quantize_w2(e, b):
            quantize(w2_codes[e][b][:], w2_bytes[e][b][:], w2_bf[e][b][:])

        h_planes = tiles([P, PACK, P], BF16, "h_planes", GROUPS)
        h_bf = tiles([P, P, PACK], BF16, "h_bf", GROUPS)
        h_codes = tiles([P, P], U32, "h_codes", GROUPS)
        h_bytes = tiles([P, P], U8, "h_bytes", GROUPS)
        y_sb = tiles([P, C], F32, "y", BLOCKS)

        def gelu(e, s):
            for t in range(PACK):
                nc.scalar.activation(h_planes[e][s][:, t, :], banks[s][t][:, :P], GELU)

        def weave_h(e, s, copy):
            round_rows(copy, h_bf[e][s][:], h_planes[e][s][:])

        def quantize_h(e, s):
            quantize(h_codes[e][s][:], h_bytes[e][s][:], h_bf[e][s][:])

        def second(e, s, b):
            acc = banks[s][b][:, :P]
            nc.tensor.matmul_mx(
                out=acc,
                lhsT=w2_codes[e][b][:].bitcast(FP8X4),
                lhsT_scale=w2_bytes[e][b][:],
                rhs=h_codes[e][s][:].bitcast(FP8X4),
                rhs_scale=h_bytes[e][s][:],
                start=True,
                stop=True,
            )
            nc.scalar.copy(y_sb[e][b][:, s * P:(s + 1) * P], acc)

        def scatter(e, b, first, count):
            nc.vector.tensor_tensor(
                result[b][:].indirect(slots(dst_sb, e * C + first, count)),
                y_sb[e][b][:, first:first + count],
                gate_sb[e][:, first:first + count],
                MULT,
            )

        def finish(e):
            round_w2(e, 0, nc.scalar.copy)
            round_w2(e, 1, nc.vector.tensor_copy)
            gelu(e, 0)
            gelu(e, 1)
            quantize_w2(e, 0)
            weave_h(e, 0, nc.vector.tensor_copy)
            quantize_w2(e, 1)
            quantize_h(e, 0)
            second(e, 0, 0)
            weave_h(e, 1, nc.scalar.copy)
            quantize_h(e, 1)
            second(e, 1, 0)
            second(e, 0, 1)
            second(e, 1, 1)
            scatter(e, 0, 0, P)
            scatter(e, 0, P, P)
            scatter(e, 1, 0, C)

        for e in range(E):
            gather_bytes(e)
        for e in range(E):
            for o in range(PASSES):
                if e == 0:
                    for expert in range(E):
                        gather_words(expert, o)
                round_w1(e, o)
                quantize_w1(e, o)
                first_pass(e, o)
            finish(e)
        for b in range(BLOCKS):
            nc.sync.dma_start(out=out[b * P:(b + 1) * P, :], in_=result[b][:])
